import numpy as np
import ml_dtypes


def mxq(x, axis, fmt="e4m3"):
    dtype, down = {"e4m3": (ml_dtypes.float8_e4m3fn, 7), "e5m2": (ml_dtypes.float8_e5m2, 14)}[fmt]
    v = np.moveaxis(np.asarray(x, np.float32).astype(ml_dtypes.bfloat16).astype(np.float64), axis, -1)
    blocks = v.reshape(v.shape[:-1] + (-1, 32))
    amax = np.abs(blocks).max(-1, keepdims=True)
    byte = np.maximum(np.where(amax > 0, np.frexp(amax)[1] - 1 + 127, 0) - down, 1)
    scale = np.exp2(byte - 127.0)
    codes = (blocks / scale).astype(np.float32).astype(dtype).astype(np.float64)
    return np.moveaxis((codes * scale).reshape(v.shape), -1, axis)


WIDE = False


def mx_kscale(k):
    if not WIDE:
        return np.ones(k)
    levels = np.array([10, -10, 5, -5, 0])
    if k % 512:
        return np.exp2(np.random.permutation(np.resize(levels, k // 32))).repeat(32)
    a = np.empty((k // 512, 16))
    for p in range(k // 512):
        a[p, :8] = np.random.permutation(np.resize(levels, 8))
        for g in range(8):
            far = levels[np.abs(levels - a[p, g]) >= 10]
            a[p, g + 8] = far[np.random.randint(len(far))]
    return np.exp2(a.ravel()).repeat(32)


def f64(x):
    return np.asarray(x).astype(np.float64)


def striped(idx):
    return np.tile(idx.reshape(-1, 16).T, (8, 1)).astype(np.uint16)


def unstriped(offs):
    return offs[:16].T.reshape(-1).astype(np.int64)


E2M1 = np.array([0.0, 0.5, 1.0, 1.5, 2.0, 3.0, 4.0, 6.0, -0.0, -0.5, -1.0, -1.5, -2.0, -3.0, -4.0, -6.0])


def pack_weight(w, fmt):
    k, n = w.shape
    w = f64(np.asarray(w, np.float32).astype(ml_dtypes.bfloat16)).reshape(k // 32, 32, n)
    amax = np.abs(w).max(1)
    if fmt == "e4m3":
        byte = np.frexp(amax)[1] - 1 + 127 - 7
    else:
        mant, ex = np.frexp(amax / 6.0)
        byte = np.where(mant > 0.5, ex, ex - 1) + 127
    byte = np.clip(np.where(amax > 0, byte, 1), 1, 254)
    scaled = (w * np.exp2(127.0 - byte)[:, None, :]).reshape(k, n).astype(np.float32)
    by_word = np.ascontiguousarray(scaled.reshape(k // 512, 128, 4, n).transpose(0, 1, 3, 2))
    if fmt == "e4m3":
        words = by_word.astype(ml_dtypes.float8_e4m3fn).view(np.uint8)
    else:
        c = by_word.astype(ml_dtypes.float4_e2m1fn).view(np.uint8) & 0xF
        words = (c[..., 0::2] | (c[..., 1::2] << 4)).reshape(k // 512, 128, 2 * n)
    return np.ascontiguousarray(words), np.ascontiguousarray(byte.astype(np.uint8).reshape(k // 512, 16, n))


def unpack_weight(words, scales, fmt):
    g, _, n = scales.shape
    words = np.ascontiguousarray(words).reshape(g, 128, n, -1)
    if fmt == "e4m3":
        vals = words.view(ml_dtypes.float8_e4m3fn).astype(np.float64)
    else:
        nib = np.empty((g, 128, n, 4), np.uint8)
        nib[..., 0::2] = words & 0xF
        nib[..., 1::2] = words >> 4
        vals = E2M1[nib]
    vals = vals * np.repeat(np.exp2(scales.astype(np.float64) - 127.0), 8, axis=1)[..., None]
    return vals.transpose(0, 1, 3, 2).reshape(g * 512, n)


def gelu(v):
    return 0.5 * v * (1.0 + np.tanh(np.sqrt(2.0 / np.pi) * (v + 0.044715 * v**3)))


K, T, S, P, H, M, N = 1024, 4096, 1024, 512, 1024, 512, 768

def setup_inputs():
    n = np.random.standard_normal
    s = mx_kscale(K)[:, None]
    u = mx_kscale(H)[:, None]
    s2 = mx_kscale(M)[:, None]
    d = {}
    d["tab_words"], d["tab_scales"] = pack_weight(n((K, T)) * s, "e2m1")
    d["offs"] = striped(np.random.permutation(T)[:S])
    d["pos1"] = striped(np.random.permutation(S)[:P])
    d["pos2"] = striped(np.random.permutation(S)[:P])
    d["w1"] = (n((K, H)) / s / K**0.5).astype(np.float32)
    d["b1"] = (0.5 * n(H)).astype(np.float32)
    d["gain"] = (np.exp(0.3 * n(H)) * u[:, 0]).astype(np.float32)
    d["w2_words"], d["w2_scales"] = pack_weight(n((H, N)) / u / H**0.5, "e2m1")
    d["swell"] = (n((M, P)) * s2).astype(np.float32)
    d["w3_words"], d["w3_scales"] = pack_weight(n((M, N)) / s2 / M**0.5, "e4m3")
    d["b2"] = (0.5 * n(N)).astype(np.float32)
    return d

def reference(tab_words, tab_scales, offs, pos1, pos2, w1, b1, gain,
              w2_words, w2_scales, swell, w3_words, w3_scales, b2):
    v = unpack_weight(tab_words, tab_scales, "e2m1")[:, unstriped(offs)]
    e = (mxq(f64(w1), 0, "e4m3").T @ v) + f64(b1)[:, None]
    gelu = 0.5 * e * (1.0 + np.tanh(0.7978845608028654 * (e + 0.044715 * e**3)))
    h = f64(gain)[:, None] * gelu
    x = h[:, unstriped(pos1)] + h[:, unstriped(pos2)]
    y = unpack_weight(w2_words, w2_scales, "e2m1").T @ mxq(x, 0, "e4m3")
    f = unpack_weight(w3_words, w3_scales, "e4m3").T @ mxq(f64(swell), 0, "e4m3")
    return np.maximum(y + f64(b2)[:, None], f)

@@ -1,0 +1,353 @@
+from contextlib import ExitStack
+
+import concourse.mybir as mybir
+
+K, T, S, PAIRS, H, M, N = 1024, 4096, 1024, 512, 1024, 512, 768
+FLOPS = 2 * (K * H * S + H * N * PAIRS + M * N * PAIRS)
+
+F32 = mybir.dt.float32
+BF16 = mybir.dt.bfloat16
+I32 = mybir.dt.int32
+U32 = mybir.dt.uint32
+U16 = mybir.dt.uint16
+U8 = mybir.dt.uint8
+FP8X4 = mybir.dt.float8_e4m3fn_x4
+FP4X4 = mybir.dt.float4_e2m1fn_x4
+ACT = mybir.ActivationFunctionType
+ALU = mybir.AluOpType
+
+P = 128
+PACK = 4
+PASS = P * PACK
+BANK = 512
+HALF = PAIRS // 2
+N_TILES = N // P
+STAGE_ROW = 16
+LAST_SPLIT = 96
+SPLIT_FROM = 5
+PIECES = ((0, 256), (256, 384), (384, 512))
+
+
+def tile_list_channel_shoal_outlook_kernel(
+    tc, tab_words, tab_scales, offs, pos1, pos2, w1, b1, gain,
+    w2_words, w2_scales, swell, w3_words, w3_scales, b2, out,
+):
+    nc = tc.nc
+    with ExitStack() as ctx:
+        keep = ctx.enter_context(tc.tile_pool(name="keep", bufs=1))
+        psum = ctx.enter_context(tc.psum_pool(name="psum", bufs=1))
+
+        def sb(name, shape, dtype, tag=None):
+            return keep.tile(shape, dtype, name=name, tag=tag or name, align_bytes=64)
+
+        def bank(index, name, shape):
+            return psum.tile(shape, F32, name=name, tag="bank%d" % index)
+
+        offs_t = keep.tile([P, S // 16], U16, name="offs_t")
+        pos1_t = keep.tile([P, PAIRS // 16], U16, name="pos1_t")
+        pos2_t = keep.tile([P, PAIRS // 16], U16, name="pos2_t")
+        tab_w = [sb("tab_w%d" % a, [P, T], U16) for a in range(2)]
+        tab_s = sb("tab_s", [P, T], U8, "pick0")
+        v_w = [sb("v_w%d" % a, [P, S], U16) for a in range(2)]
+        v_s = [sb("v_s%d" % a, [P, S], U8) for a in range(2)]
+        w_s = sb("w_s", [P, 3, N], U8)
+        b1_t = sb("b1_t", [P, 2 * PACK], F32)
+        gain_t = sb("gain_t", [P, 2 * PACK], F32)
+        b2_t = sb("b2_t", [P, N_TILES], F32)
+        w2_w = sb("w2_w", [P, 2, 2 * N], U8)
+        w3_w = sb("w3_w", [P, N], U32)
+
+        nc.vector.memset(tab_s[:].bitcast(I32), 0)
+        nc.vector.memset(w_s[:].rearrange("p a n -> p (a n)").bitcast(I32), 0)
+        nc.vector.memset(v_s[1][:].bitcast(I32), 0)
+
+        def load_w1(a, b, c0, width, tag=None):
+            raw = sb("w1_raw%d%d_%d" % (a, b, c0), [P, PACK, width], F32, tag)
+            rows = w1[a * PASS : (a + 1) * PASS, b * PASS + c0 : b * PASS + c0 + width]
+            nc.sync.dma_start(out=raw[:], in_=rows.rearrange("(p j) c -> p j c", j=PACK))
+            return raw
+
+        def load_per_row(tile, vec):
+            nc.sync.dma_start(
+                out=tile[:].rearrange("p (b t) -> p b t", t=PACK),
+                in_=vec.rearrange("(b p t) -> p b t", p=P, t=PACK),
+            )
+
+        nc.sync.dma_start(offs_t[:], offs)
+        nc.sync.dma_start(out=tab_w[0][:].bitcast(I32), in_=tab_words[0].bitcast(I32))
+        by_row = tab_scales.rearrange("a (q r) t -> r q a t", r=4)
+        for r in range(4):
+            nc.sync.dma_start(out=tab_s[r:P:STAGE_ROW, :].bitcast(I32), in_=by_row[r].bitcast(I32))
+        raw00 = load_w1(0, 0, 0, PASS)
+        nc.sync.dma_start(out=tab_w[1][:].bitcast(I32), in_=tab_words[1].bitcast(I32))
+        raw10 = [load_w1(1, 0, c0, PASS // 2) for c0 in (0, PASS // 2)]
+        load_per_row(b1_t, b1)
+        nc.sync.dma_start(pos1_t[:], pos1)
+        nc.sync.dma_start(pos2_t[:], pos2)
+        for q in range(4):
+            nc.gpsimd.dma_start(
+                out=w_s[32 * q : 32 * q + 4, 2, :].bitcast(I32),
+                in_=w3_scales[0, 4 * q : 4 * q + 4, :].bitcast(I32),
+            )
+        for q in range(4):
+            nc.gpsimd.dma_start(
+                out=w_s[32 * q : 32 * q + 4, 0:2, :].bitcast(I32),
+                in_=w2_scales[:, 4 * q : 4 * q + 4, :].rearrange("a r n -> r a n").bitcast(I32),
+            )
+
+        def gather_table(dst, window):
+            nc.vector.tensor_copy(dst[:], window[:].indirect(offs_t[:]))
+
+        gather_table(v_w[0], tab_w[0])
+        gather_table(v_s[0], tab_s)
+        gather_table(v_w[1], tab_w[1])
+        nc.sync.dma_start(
+            out=v_s[1][0 : P - STAGE_ROW, :].bitcast(I32), in_=v_s[0][STAGE_ROW:P, :].bitcast(I32)
+        )
+        swell_raw = sb("swell_raw", [P, PACK, PAIRS], F32, "pick0")
+        nc.sync.dma_start(out=swell_raw[:], in_=swell.rearrange("(p j) c -> p j c", j=PACK))
+        raw01 = load_w1(0, 1, 0, PASS)
+        raw11 = load_w1(1, 1, 0, PASS)
+        nc.sync.dma_start(
+            out=w3_w[:].bitcast(I32), in_=w3_words[0].rearrange("p n t -> p (n t)").bitcast(I32)
+        )
+        load_per_row(gain_t, gain)
+        nc.sync.dma_start(
+            out=w2_w[:].bitcast(I32), in_=w2_words.rearrange("a p c -> p a c").bitcast(I32)
+        )
+        with nc.allow_non_contiguous_dma(reason="one bias value for each output row"):
+            nc.sync.dma_start(out=b2_t[:], in_=b2.rearrange("(i p) -> p i", p=P))
+
+        w1_g = {}
+        w1_c = {}
+        w1_s = {}
+        for a in range(2):
+            for b in range(2):
+                w1_g.setdefault((a, b), sb("w1_g%d%d" % (a, b), [P, PACK * PASS], BF16))
+                w1_c.setdefault((a, b), sb("w1_c%d%d" % (a, b), [P, PASS], U32))
+                w1_s.setdefault((a, b), sb("w1_s%d%d" % (a, b), [P, PASS], U8))
+
+        def scalar_round(out, in_):
+            nc.scalar.activation(out=out, in_=in_, func=ACT.Copy)
+
+        def group_w1(copy, a, b, raw, c0, lo, hi):
+            dst = w1_g[a, b][:].rearrange("p (t m j) -> p m j t", t=PACK, j=PACK)
+            copy(
+                out=dst[:, (c0 + lo) // PACK : (c0 + hi) // PACK],
+                in_=raw[:, :, lo:hi].rearrange("p j (m t) -> p m j t", t=PACK),
+            )
+
+        def quantize(codes, scales, grouped, lo, hi):
+            nc.vector.quantize_mx(
+                out=codes[:, lo:hi].bitcast(FP8X4),
+                scales=scales[:, lo:hi],
+                in_=grouped[:, PACK * lo : PACK * hi],
+            )
+
+        def quantize_w1(a, b, lo, hi):
+            quantize(w1_c[a, b], w1_s[a, b], w1_g[a, b], lo, hi)
+
+        def interleave(copy, grouped, planes):
+            copy(
+                out=grouped.rearrange("p (c i t) -> p c t i", i=4, t=PACK),
+                in_=planes.rearrange("p t (c i) -> p c t i", i=4),
+            )
+
+        gelu_t = [sb("gelu%d" % s, [P, S], F32) for s in range(2 * PACK)]
+
+        def first_stage(s):
+            b, t = divmod(s, PACK)
+            cols = slice(t * P, (t + 1) * P)
+            accs = [bank(2 * (s % 2) + u, "e%d_%d" % (s, u), [P, BANK]) for u in range(2)]
+            for a in ((0, 1), (1, 0))[b]:
+                for u in range(2):
+                    nc.tensor.matmul_mx(
+                        out=accs[u][:],
+                        lhsT=w1_c[a, b][:, cols].bitcast(FP8X4),
+                        lhsT_scale=w1_s[a, b][:, cols],
+                        rhs=v_w[a][:, u * BANK : (u + 1) * BANK].bitcast(FP4X4),
+                        rhs_scale=v_s[a][:, u * BANK : (u + 1) * BANK],
+                        start=(a == b),
+                        stop=(a != b),
+                    )
+            for u in range(2):
+                nc.scalar.activation(
+                    out=gelu_t[s][:, u * BANK : (u + 1) * BANK],
+                    in_=accs[u][:],
+                    func=ACT.Gelu_apprx_tanh,
+                    bias=b1_t[:, s : s + 1],
+                )
+
+        sums = {}
+        x_planes = {}
+        sums_tag = {1: "w1_g01", 2: "w1_g11"}
+        x_g = {}
+        x_c = [sb("x_c%d" % b, [P, PAIRS], U32) for b in range(2)]
+        x_s = [sb("x_s%d" % b, [P, PAIRS], U8) for b in range(2)]
+
+        def pick_first(s, lo, hi, picked):
+            nc.vector.tensor_copy(picked, gelu_t[s][:].indirect(pos1_t[:, lo // 16 : hi // 16]))
+
+        def pick_second(s, lo, hi, picked):
+            if s not in sums:
+                sums.setdefault(s, sb("sums%d" % s, [P, PAIRS], F32, sums_tag.get(s)))
+            nc.vector.tensor_tensor(
+                sums[s][:, lo:hi],
+                gelu_t[s][:].indirect(pos2_t[:, lo // 16 : hi // 16]),
+                picked,
+                ALU.add,
+            )
+
+        def pick_pairs(units, tags=("pick0", "pick1")):
+            for first, second in zip(units[0::2], units[1::2]):
+                width = first[2] - first[1]
+                name = "picked%d_%d" % first[:2]
+                if len(tags) == 1:
+                    both = sb(name, [P, 2, width], F32, tags[0])
+                    held = [both[:, 0, :], both[:, 1, :]]
+                else:
+                    held = [sb(name + tag, [P, width], F32, tag)[:] for tag in tags]
+                pick_first(*first, held[0])
+                pick_first(*second, held[1])
+                pick_second(*first, held[0])
+                pick_second(*second, held[1])
+
+        def in_two(s, lo, hi):
+            mid = (lo + hi) // 2
+            return [(s, lo, mid), (s, mid, hi)]
+
+        def apply_gain(s, lo, hi):
+            b, t = divmod(s, PACK)
+            if b not in x_planes:
+                tag = "w1_raw11_0" if b == 0 else None
+                x_planes.setdefault(b, sb("x_planes%d" % b, [P, PACK, PAIRS], BF16, tag))
+            nc.scalar.activation(
+                out=x_planes[b][:, t, lo:hi],
+                in_=sums[s][:, lo:hi],
+                func=ACT.Copy,
+                scale=gain_t[:, s : s + 1],
+            )
+
+        def group_x(b, lo, hi):
+            x_g.setdefault((b, lo), sb("x_g%d_%d" % (b, lo), [P, PACK * (hi - lo)], BF16))
+            interleave(nc.scalar.copy, x_g[b, lo][:], x_planes[b][:, :, lo:hi])
+
+        def quantize_x(b, lo, hi):
+            quantize(x_c[b][:, lo:hi], x_s[b][:, lo:hi], x_g[b, lo], 0, hi - lo)
+
+        swell_g = sb("swell_g", [P, PACK * PAIRS], BF16, "pick1")
+        swell_c = sb("swell_c", [P, PAIRS], U32)
+        swell_s = sb("swell_s", [P, PAIRS], U8)
+        f_t = [sb("f%d" % i, [P, PAIRS], F32) for i in range(N_TILES)]
+
+        def swell_features(i):
+            acc = bank((4, 5, 6, 7, 2, 3)[i], "f_acc%d" % i, [P, PAIRS])
+            nc.tensor.matmul_mx(
+                out=acc[:],
+                lhsT=w3_w[:, i * P : (i + 1) * P].bitcast(FP8X4),
+                lhsT_scale=w_s[:, 2, i * P : (i + 1) * P],
+                rhs=swell_c[:].bitcast(FP8X4),
+                rhs_scale=swell_s[:],
+                start=True,
+                stop=True,
+            )
+            nc.scalar.copy(out=f_t[i][:], in_=acc[:])
+
+        y_acc = {}
+        y_banks = [4, 5, 6, 7, 0, 1, 2, 3]
+
+        def tiles_per_bank(lo, hi):
+            return 2 if hi - lo == HALF else 3
+
+        def second_stage(b, lo, hi):
+            per = tiles_per_bank(lo, hi)
+            for g in range(N_TILES // per):
+                if b == 0:
+                    acc = bank(y_banks[len(y_acc)], "y%d_%d" % (lo, g), [P, per, hi - lo])
+                    y_acc.setdefault((lo, g), acc)
+                for u in range(per):
+                    i = per * g + u
+                    nc.tensor.matmul_mx(
+                        out=y_acc[lo, g][:, u, :],
+                        lhsT=w2_w[:, b, 2 * i * P : 2 * (i + 1) * P].bitcast(FP4X4),
+                        lhsT_scale=w_s[:, b, i * P : (i + 1) * P],
+                        rhs=x_c[b][:, lo:hi].bitcast(FP8X4),
+                        rhs_scale=x_s[b][:, lo:hi],
+                        start=(b == 0 and u == 0),
+                        stop=(b == 1 and u == per - 1),
+                    )
+
+        def finish(lo, hi):
+            per = tiles_per_bank(lo, hi)
+            for g in range(N_TILES // per):
+                res = sb("res%d_%d" % (lo, g), [P, per, hi - lo], F32)
+                for u in range(per):
+                    i = per * g + u
+                    nc.vector.scalar_tensor_tensor(
+                        out=res[:, u, :],
+                        in0=y_acc[lo, g][:, u, :],
+                        scalar=b2_t[:, i : i + 1],
+                        in1=f_t[i][:, lo:hi],
+                        op0=ALU.add,
+                        op1=ALU.max,
+                    )
+                rows = out[per * g * P : per * (g + 1) * P, lo:hi]
+                nc.sync.dma_start(out=rows.rearrange("(u p) c -> p u c", p=P), in_=res[:])
+
+        group_w1(scalar_round, 0, 0, raw00, 0, 0, PASS)
+        group_w1(scalar_round, 1, 0, raw10[0], 0, 0, PASS // 2)
+        quantize_w1(0, 0, 0, P)
+        group_w1(scalar_round, 1, 0, raw10[1], PASS // 2, 0, LAST_SPLIT)
+        group_w1(nc.vector.tensor_copy, 1, 0, raw10[1], PASS // 2, LAST_SPLIT, PASS // 2)
+        quantize_w1(1, 0, 0, P)
+        quantize_w1(0, 0, P, PASS)
+        quantize_w1(1, 0, P, PASS)
+
+        first_stage(0)
+        interleave(nc.vector.tensor_copy, swell_g[:], swell_raw[:])
+        quantize(swell_c, swell_s, swell_g, 0, PAIRS)
+        first_stage(1)
+        pick_pairs(in_two(0, 0, PAIRS))
+        first_stage(2)
+        first_stage(3)
+        group_w1(nc.vector.tensor_copy, 0, 1, raw01, 0, 0, PASS)
+        quantize_w1(0, 1, 0, PASS)
+        group_w1(scalar_round, 1, 1, raw11, 0, 0, PASS)
+        pick_pairs(in_two(1, 0, PAIRS))
+        quantize_w1(1, 1, 0, PASS)
+        pick_pairs(in_two(2, 0, PAIRS))
+        for i in range(N_TILES):
+            swell_features(i)
+        for s in range(PACK - 1):
+            apply_gain(s, 0, PAIRS)
+        pick_pairs(in_two(3, 0, PAIRS))
+        for s in range(PACK, 2 * PACK):
+            first_stage(s)
+        apply_gain(3, 0, PAIRS)
+        group_x(0, 0, PAIRS)
+        for s in range(PACK, SPLIT_FROM):
+            pick_pairs(in_two(s, 0, PAIRS))
+        for s in range(PACK, SPLIT_FROM):
+            apply_gain(s, 0, PAIRS)
+        late = range(SPLIT_FROM, 2 * PACK)
+
+        def close_piece(lo, hi):
+            for s in late:
+                apply_gain(s, lo, hi)
+            group_x(1, lo, hi)
+            quantize_x(1, lo, hi)
+            second_stage(1, lo, hi)
+
+        pick_pairs([unit for s in late for unit in in_two(s, *PIECES[0])])
+        rest = [(s, lo, hi) for lo, hi in PIECES[1:] for s in late]
+        pick_pairs(rest[0:2])
+        quantize_x(0, 0, PAIRS)
+        for piece in PIECES:
+            second_stage(0, *piece)
+        pick_pairs(rest[2:4], ("x_g0_0", "w1_raw11_0"))
+        close_piece(*PIECES[0])
+        pick_pairs(rest[4:6], ("x_g1_0",))
+        close_piece(*PIECES[1])
+        close_piece(*PIECES[2])
+        for piece in PIECES:
+            finish(*piece)

@@ -22,9 +22,7 @@ PASS = P * PACK
 BANK = 512
 HALF = PAIRS // 2
 N_TILES = N // P
-STAGE_ROW = 16
-LAST_SPLIT = 96
-SPLIT_FROM = 5
+X_SPLIT = 256
 PIECES = ((0, 256), (256, 384), (384, 512))
 
 
@@ -47,11 +45,11 @@ def tile_list_channel_shoal_outlook_kernel(
         pos1_t = keep.tile([P, PAIRS // 16], U16, name="pos1_t")
         pos2_t = keep.tile([P, PAIRS // 16], U16, name="pos2_t")
         tab_w = [sb("tab_w%d" % a, [P, T], U16) for a in range(2)]
-        tab_s = sb("tab_s", [P, T], U8, "pick0")
-        v_w = [sb("v_w%d" % a, [P, S], U16) for a in range(2)]
-        v_s = [sb("v_s%d" % a, [P, S], U8) for a in range(2)]
+        tab_s = sb("tab_s", [P, T], U8)
+        v_rows = sb("v_rows", [P, S], U8)
+        v_s = sb("v_s", [P, 2, S], U8)
         w_s = sb("w_s", [P, 3, N], U8)
-        b1_t = sb("b1_t", [P, 2 * PACK], F32)
+        b1_t = [sb("b1_%d" % k, [P, 2], F32) for k in range(PACK)]
         gain_t = sb("gain_t", [P, 2 * PACK], F32)
         b2_t = sb("b2_t", [P, N_TILES], F32)
         w2_w = sb("w2_w", [P, 2, 2 * N], U8)
@@ -59,7 +57,7 @@ def tile_list_channel_shoal_outlook_kernel(
 
         nc.vector.memset(tab_s[:].bitcast(I32), 0)
         nc.vector.memset(w_s[:].rearrange("p a n -> p (a n)").bitcast(I32), 0)
-        nc.vector.memset(v_s[1][:].bitcast(I32), 0)
+        nc.vector.memset(v_s[:].rearrange("p a n -> p (a n)").bitcast(I32), 0)
 
         def load_w1(a, b, c0, width, tag=None):
             raw = sb("w1_raw%d%d_%d" % (a, b, c0), [P, PACK, width], F32, tag)
@@ -73,40 +71,50 @@ def tile_list_channel_shoal_outlook_kernel(
                 in_=vec.rearrange("(b p t) -> p b t", p=P, t=PACK),
             )
 
+        def load_bias(k):
+            b, half = divmod(k, 2)
+            by_row = b1.rearrange("(b p t) -> b p t", p=P, t=PACK)
+            nc.sync.dma_start(out=b1_t[k][:], in_=by_row[b, :, 2 * half : 2 * half + 2])
+
         nc.sync.dma_start(offs_t[:], offs)
         nc.sync.dma_start(out=tab_w[0][:].bitcast(I32), in_=tab_words[0].bitcast(I32))
-        by_row = tab_scales.rearrange("a (q r) t -> r q a t", r=4)
-        for r in range(4):
-            nc.sync.dma_start(out=tab_s[r:P:STAGE_ROW, :].bitcast(I32), in_=by_row[r].bitcast(I32))
-        raw00 = load_w1(0, 0, 0, PASS)
-        nc.sync.dma_start(out=tab_w[1][:].bitcast(I32), in_=tab_words[1].bitcast(I32))
-        raw10 = [load_w1(1, 0, c0, PASS // 2) for c0 in (0, PASS // 2)]
-        load_per_row(b1_t, b1)
+        nc.sync.dma_start(
+            out=tab_s[0:P:4, :].bitcast(I32),
+            in_=tab_scales.rearrange("a q t -> (a q) t").bitcast(I32),
+        )
         nc.sync.dma_start(pos1_t[:], pos1)
         nc.sync.dma_start(pos2_t[:], pos2)
-        for q in range(4):
-            nc.gpsimd.dma_start(
-                out=w_s[32 * q : 32 * q + 4, 2, :].bitcast(I32),
-                in_=w3_scales[0, 4 * q : 4 * q + 4, :].bitcast(I32),
-            )
-        for q in range(4):
-            nc.gpsimd.dma_start(
-                out=w_s[32 * q : 32 * q + 4, 0:2, :].bitcast(I32),
-                in_=w2_scales[:, 4 * q : 4 * q + 4, :].rearrange("a r n -> r a n").bitcast(I32),
-            )
+        load_bias(0)
+        raw00 = load_w1(0, 0, 0, PASS)
+        nc.sync.dma_start(out=tab_w[1][:].bitcast(I32), in_=tab_words[1].bitcast(I32))
+        raw10 = [load_w1(1, 0, 0, PASS // 2)]
+        raw10.append(load_w1(1, 0, PASS // 2, PASS // 2))
 
         def gather_table(dst, window):
             nc.vector.tensor_copy(dst[:], window[:].indirect(offs_t[:]))
 
+        gather_table(v_rows, tab_s)
+        v_w = [sb("v_w%d" % a, [P, S], U16, ("tab_s", None)[a]) for a in range(2)]
         gather_table(v_w[0], tab_w[0])
-        gather_table(v_s[0], tab_s)
         gather_table(v_w[1], tab_w[1])
-        nc.sync.dma_start(
-            out=v_s[1][0 : P - STAGE_ROW, :].bitcast(I32), in_=v_s[0][STAGE_ROW:P, :].bitcast(I32)
-        )
+        for n in range(8):
+            a, q = divmod(n, 4)
+            queue = nc.sync if n < 6 else nc.gpsimd
+            queue.dma_start(
+                out=v_s[32 * q : 32 * q + 4, a, :].bitcast(I32),
+                in_=v_rows[64 * a + 16 * q : 64 * a + 16 * q + 16 : 4, :].bitcast(I32),
+            )
         swell_raw = sb("swell_raw", [P, PACK, PAIRS], F32, "pick0")
         nc.sync.dma_start(out=swell_raw[:], in_=swell.rearrange("(p j) c -> p j c", j=PACK))
+        load_bias(1)
         raw01 = load_w1(0, 1, 0, PASS)
+        load_bias(2)
+        load_bias(3)
+        for q in range(4):
+            nc.sync.dma_start(
+                out=w_s[32 * q : 32 * q + 4, 2, :].bitcast(I32),
+                in_=w3_scales[0, 4 * q : 4 * q + 4, :].bitcast(I32),
+            )
         raw11 = load_w1(1, 1, 0, PASS)
         nc.sync.dma_start(
             out=w3_w[:].bitcast(I32), in_=w3_words[0].rearrange("p n t -> p (n t)").bitcast(I32)
@@ -115,6 +123,11 @@ def tile_list_channel_shoal_outlook_kernel(
         nc.sync.dma_start(
             out=w2_w[:].bitcast(I32), in_=w2_words.rearrange("a p c -> p a c").bitcast(I32)
         )
+        for q in range(4):
+            nc.sync.dma_start(
+                out=w_s[32 * q : 32 * q + 4, 0:2, :].bitcast(I32),
+                in_=w2_scales[:, 4 * q : 4 * q + 4, :].rearrange("a r n -> r a n").bitcast(I32),
+            )
         with nc.allow_non_contiguous_dma(reason="one bias value for each output row"):
             nc.sync.dma_start(out=b2_t[:], in_=b2.rearrange("(i p) -> p i", p=P))
 
@@ -131,10 +144,10 @@ def tile_list_channel_shoal_outlook_kernel(
             nc.scalar.activation(out=out, in_=in_, func=ACT.Copy)
 
         def group_w1(copy, a, b, raw, c0, lo, hi):
-            dst = w1_g[a, b][:].rearrange("p (t m j) -> p m j t", t=PACK, j=PACK)
+            dst = w1_g[a, b][:].rearrange("p (t m j) -> p m t j", t=PACK, j=PACK)
             copy(
                 out=dst[:, (c0 + lo) // PACK : (c0 + hi) // PACK],
-                in_=raw[:, :, lo:hi].rearrange("p j (m t) -> p m j t", t=PACK),
+                in_=raw[:, :, lo:hi].rearrange("p j (m t) -> p m t j", t=PACK),
             )
 
         def quantize(codes, scales, grouped, lo, hi):
@@ -159,89 +172,82 @@ def tile_list_channel_shoal_outlook_kernel(
             b, t = divmod(s, PACK)
             cols = slice(t * P, (t + 1) * P)
             accs = [bank(2 * (s % 2) + u, "e%d_%d" % (s, u), [P, BANK]) for u in range(2)]
-            for a in ((0, 1), (1, 0))[b]:
-                for u in range(2):
+            if s == 0:
+                order = [(a, u) for a in (0, 1) for u in range(2)]
+            else:
+                order = [(a, u) for u in range(2) for a in (1, 0)]
+            for a, u in order:
+                if True:
                     nc.tensor.matmul_mx(
                         out=accs[u][:],
                         lhsT=w1_c[a, b][:, cols].bitcast(FP8X4),
                         lhsT_scale=w1_s[a, b][:, cols],
                         rhs=v_w[a][:, u * BANK : (u + 1) * BANK].bitcast(FP4X4),
-                        rhs_scale=v_s[a][:, u * BANK : (u + 1) * BANK],
-                        start=(a == b),
-                        stop=(a != b),
+                        rhs_scale=v_s[:, a, u * BANK : (u + 1) * BANK],
+                        start=(a == order[0][0]),
+                        stop=(a != order[0][0]),
                     )
             for u in range(2):
                 nc.scalar.activation(
                     out=gelu_t[s][:, u * BANK : (u + 1) * BANK],
                     in_=accs[u][:],
                     func=ACT.Gelu_apprx_tanh,
-                    bias=b1_t[:, s : s + 1],
+                    bias=b1_t[s // 2][:, s % 2 : s % 2 + 1],
                 )
 
         sums = {}
         x_planes = {}
-        sums_tag = {1: "w1_g01", 2: "w1_g11"}
         x_g = {}
         x_c = [sb("x_c%d" % b, [P, PAIRS], U32) for b in range(2)]
         x_s = [sb("x_s%d" % b, [P, PAIRS], U8) for b in range(2)]
 
-        def pick_first(s, lo, hi, picked):
-            nc.vector.tensor_copy(picked, gelu_t[s][:].indirect(pos1_t[:, lo // 16 : hi // 16]))
+        def pick_first(k, lo, hi, tag):
+            picked = sb("picked%d_%d" % (k, lo), [P, 2, hi - lo], F32, tag)
+            for u in range(2):
+                window = gelu_t[2 * k + u][:]
+                nc.vector.tensor_copy(picked[:, u, :], window.indirect(pos1_t[:, lo // 16 : hi // 16]))
+            return picked
 
-        def pick_second(s, lo, hi, picked):
-            if s not in sums:
-                sums.setdefault(s, sb("sums%d" % s, [P, PAIRS], F32, sums_tag.get(s)))
-            nc.vector.tensor_tensor(
-                sums[s][:, lo:hi],
-                gelu_t[s][:].indirect(pos2_t[:, lo // 16 : hi // 16]),
-                picked,
-                ALU.add,
-            )
-
-        def pick_pairs(units, tags=("pick0", "pick1")):
-            for first, second in zip(units[0::2], units[1::2]):
-                width = first[2] - first[1]
-                name = "picked%d_%d" % first[:2]
-                if len(tags) == 1:
-                    both = sb(name, [P, 2, width], F32, tags[0])
-                    held = [both[:, 0, :], both[:, 1, :]]
-                else:
-                    held = [sb(name + tag, [P, width], F32, tag)[:] for tag in tags]
-                pick_first(*first, held[0])
-                pick_first(*second, held[1])
-                pick_second(*first, held[0])
-                pick_second(*second, held[1])
-
-        def in_two(s, lo, hi):
-            mid = (lo + hi) // 2
-            return [(s, lo, mid), (s, mid, hi)]
+        def pick_second(k, lo, hi, picked, tag):
+            total = sb("sums%d_%d" % (k, lo), [P, 2, hi - lo], F32, tag)
+            for u in range(2):
+                window = gelu_t[2 * k + u][:]
+                nc.vector.tensor_tensor(
+                    total[:, u, :],
+                    window.indirect(pos2_t[:, lo // 16 : hi // 16]),
+                    picked[:, u, :],
+                    ALU.add,
+                )
+                sums.setdefault((2 * k + u, lo), total[:, u, :])
 
         def apply_gain(s, lo, hi):
             b, t = divmod(s, PACK)
-            if b not in x_planes:
-                tag = "w1_raw11_0" if b == 0 else None
-                x_planes.setdefault(b, sb("x_planes%d" % b, [P, PACK, PAIRS], BF16, tag))
+            base = lo if (s, lo) in sums else 0
+            if (b, lo) not in x_planes:
+                name = "x_planes%d_%d" % (b, lo)
+                tile = sb(name, [P, PACK, hi - lo], BF16, "w1_g11" if b == 0 else None)
+                x_planes.setdefault((b, lo), tile)
             nc.scalar.activation(
-                out=x_planes[b][:, t, lo:hi],
-                in_=sums[s][:, lo:hi],
+                out=x_planes[b, lo][:, t, :],
+                in_=sums[s, base][:, lo - base : hi - base],
                 func=ACT.Copy,
                 scale=gain_t[:, s : s + 1],
             )
 
-        def group_x(b, lo, hi):
+        def group_x(copy, b, lo, hi):
             x_g.setdefault((b, lo), sb("x_g%d_%d" % (b, lo), [P, PACK * (hi - lo)], BF16))
-            interleave(nc.scalar.copy, x_g[b, lo][:], x_planes[b][:, :, lo:hi])
+            interleave(copy, x_g[b, lo][:], x_planes[b, lo][:])
 
         def quantize_x(b, lo, hi):
             quantize(x_c[b][:, lo:hi], x_s[b][:, lo:hi], x_g[b, lo], 0, hi - lo)
 
-        swell_g = sb("swell_g", [P, PACK * PAIRS], BF16, "pick1")
+        swell_g = sb("swell_g", [P, PACK * PAIRS], BF16)
         swell_c = sb("swell_c", [P, PAIRS], U32)
         swell_s = sb("swell_s", [P, PAIRS], U8)
         f_t = [sb("f%d" % i, [P, PAIRS], F32) for i in range(N_TILES)]
 
         def swell_features(i):
-            acc = bank((4, 5, 6, 7, 2, 3)[i], "f_acc%d" % i, [P, PAIRS])
+            acc = bank(4 + i % 4, "f_acc%d" % i, [P, PAIRS])
             nc.tensor.matmul_mx(
                 out=acc[:],
                 lhsT=w3_w[:, i * P : (i + 1) * P].bitcast(FP8X4),
@@ -254,100 +260,91 @@ def tile_list_channel_shoal_outlook_kernel(
             nc.scalar.copy(out=f_t[i][:], in_=acc[:])
 
         y_acc = {}
-        y_banks = [4, 5, 6, 7, 0, 1, 2, 3]
-
-        def tiles_per_bank(lo, hi):
-            return 2 if hi - lo == HALF else 3
+        y_banks = (4, 5, 6, 7, 0, 2)
 
         def second_stage(b, lo, hi):
-            per = tiles_per_bank(lo, hi)
-            for g in range(N_TILES // per):
+            h = lo // HALF
+            for g in range(N_TILES // 2):
                 if b == 0:
-                    acc = bank(y_banks[len(y_acc)], "y%d_%d" % (lo, g), [P, per, hi - lo])
-                    y_acc.setdefault((lo, g), acc)
-                for u in range(per):
-                    i = per * g + u
+                    acc = bank(y_banks[3 * h + g], "y%d_%d" % (h, g), [P, 2, HALF])
+                    y_acc.setdefault((h, g), acc)
+                for u in range(2):
+                    i = 2 * g + u
                     nc.tensor.matmul_mx(
-                        out=y_acc[lo, g][:, u, :],
+                        out=y_acc[h, g][:, u, lo - h * HALF : hi - h * HALF],
                         lhsT=w2_w[:, b, 2 * i * P : 2 * (i + 1) * P].bitcast(FP4X4),
                         lhsT_scale=w_s[:, b, i * P : (i + 1) * P],
                         rhs=x_c[b][:, lo:hi].bitcast(FP8X4),
                         rhs_scale=x_s[b][:, lo:hi],
                         start=(b == 0 and u == 0),
-                        stop=(b == 1 and u == per - 1),
+                        stop=(b == 1 and u == 1 and hi % HALF == 0),
                     )
 
-        def finish(lo, hi):
-            per = tiles_per_bank(lo, hi)
-            for g in range(N_TILES // per):
-                res = sb("res%d_%d" % (lo, g), [P, per, hi - lo], F32)
-                for u in range(per):
-                    i = per * g + u
-                    nc.vector.scalar_tensor_tensor(
-                        out=res[:, u, :],
-                        in0=y_acc[lo, g][:, u, :],
-                        scalar=b2_t[:, i : i + 1],
-                        in1=f_t[i][:, lo:hi],
-                        op0=ALU.add,
-                        op1=ALU.max,
-                    )
-                rows = out[per * g * P : per * (g + 1) * P, lo:hi]
-                nc.sync.dma_start(out=rows.rearrange("(u p) c -> p u c", p=P), in_=res[:])
+        def finish(h):
+            cols = slice(h * HALF, (h + 1) * HALF)
+            for i in range(N_TILES):
+                res = sb("res%d_%d" % (h, i), [P, HALF], F32)
+                nc.vector.scalar_tensor_tensor(
+                    out=res[:],
+                    in0=y_acc[h, i // 2][:, i % 2, :],
+                    scalar=b2_t[:, i : i + 1],
+                    in1=f_t[i][:, cols],
+                    op0=ALU.add,
+                    op1=ALU.max,
+                )
+                nc.sync.dma_start(out=out[i * P : (i + 1) * P, cols], in_=res[:])
 
         group_w1(scalar_round, 0, 0, raw00, 0, 0, PASS)
         group_w1(scalar_round, 1, 0, raw10[0], 0, 0, PASS // 2)
         quantize_w1(0, 0, 0, P)
-        group_w1(scalar_round, 1, 0, raw10[1], PASS // 2, 0, LAST_SPLIT)
-        group_w1(nc.vector.tensor_copy, 1, 0, raw10[1], PASS // 2, LAST_SPLIT, PASS // 2)
+        group_w1(nc.vector.tensor_copy, 1, 0, raw10[1], PASS // 2, 0, PASS // 2)
         quantize_w1(1, 0, 0, P)
         quantize_w1(0, 0, P, PASS)
         quantize_w1(1, 0, P, PASS)
 
         first_stage(0)
         interleave(nc.vector.tensor_copy, swell_g[:], swell_raw[:])
-        quantize(swell_c, swell_s, swell_g, 0, PAIRS)
         first_stage(1)
-        pick_pairs(in_two(0, 0, PAIRS))
+        picked = pick_first(0, 0, PAIRS, "pick0")
+        quantize(swell_c, swell_s, swell_g, 0, PAIRS)
+        pick_second(0, 0, PAIRS, picked, None)
         first_stage(2)
         first_stage(3)
-        group_w1(nc.vector.tensor_copy, 0, 1, raw01, 0, 0, PASS)
+        picked = pick_first(1, 0, PAIRS, None)
+        group_w1(scalar_round, 0, 1, raw01, 0, 0, PASS)
         quantize_w1(0, 1, 0, PASS)
         group_w1(scalar_round, 1, 1, raw11, 0, 0, PASS)
-        pick_pairs(in_two(1, 0, PAIRS))
         quantize_w1(1, 1, 0, PASS)
-        pick_pairs(in_two(2, 0, PAIRS))
+        pick_second(1, 0, PAIRS, picked, "w1_raw11_0")
+        first_stage(4)
+        first_stage(5)
+        pick_second(2, 0, PAIRS, pick_first(2, 0, PAIRS, None), "b1_2")
         for i in range(N_TILES):
             swell_features(i)
-        for s in range(PACK - 1):
+        first_stage(6)
+        first_stage(7)
+        for s in range(PACK):
             apply_gain(s, 0, PAIRS)
-        pick_pairs(in_two(3, 0, PAIRS))
-        for s in range(PACK, 2 * PACK):
-            first_stage(s)
-        apply_gain(3, 0, PAIRS)
-        group_x(0, 0, PAIRS)
-        for s in range(PACK, SPLIT_FROM):
-            pick_pairs(in_two(s, 0, PAIRS))
-        for s in range(PACK, SPLIT_FROM):
-            apply_gain(s, 0, PAIRS)
-        late = range(SPLIT_FROM, 2 * PACK)
+        pick_second(3, *PIECES[0], pick_first(3, *PIECES[0], None), "b1_3")
+        x_g.setdefault((0, 0), sb("x_g0_0", [P, PACK * PAIRS], BF16))
+        cut = X_SPLIT
+        interleave(nc.scalar.copy, x_g[0, 0][:, : PACK * cut], x_planes[0, 0][:, :, :cut])
+        interleave(nc.vector.tensor_copy, x_g[0, 0][:, PACK * cut :], x_planes[0, 0][:, :, cut:])
+        quantize_x(0, 0, PAIRS)
+        for h in range(2):
+            second_stage(0, h * HALF, (h + 1) * HALF)
 
-        def close_piece(lo, hi):
-            for s in late:
+        def close_piece(copy, lo, hi):
+            for s in range(PACK, 2 * PACK):
                 apply_gain(s, lo, hi)
-            group_x(1, lo, hi)
+            group_x(copy, 1, lo, hi)
             quantize_x(1, lo, hi)
             second_stage(1, lo, hi)
 
-        pick_pairs([unit for s in late for unit in in_two(s, *PIECES[0])])
-        rest = [(s, lo, hi) for lo, hi in PIECES[1:] for s in late]
-        pick_pairs(rest[0:2])
-        quantize_x(0, 0, PAIRS)
-        for piece in PIECES:
-            second_stage(0, *piece)
-        pick_pairs(rest[2:4], ("x_g0_0", "w1_raw11_0"))
-        close_piece(*PIECES[0])
-        pick_pairs(rest[4:6], ("x_g1_0",))
-        close_piece(*PIECES[1])
-        close_piece(*PIECES[2])
-        for piece in PIECES:
-            finish(*piece)
+        pick_second(3, *PIECES[1], pick_first(3, *PIECES[1], "w1_g11"), None)
+        close_piece(nc.scalar.copy, *PIECES[0])
+        pick_second(3, *PIECES[2], pick_first(3, *PIECES[2], "x_planes1_0"), None)
+        close_piece(nc.scalar.copy, *PIECES[1])
+        close_piece(nc.scalar.copy, *PIECES[2])
+        for h in range(2):
+            finish(h)

@@ -22,7 +22,6 @@ PASS = P * PACK
 BANK = 512
 HALF = PAIRS // 2
 N_TILES = N // P
-X_SPLIT = 256
 PIECES = ((0, 256), (256, 384), (384, 512))
 
 
@@ -104,22 +103,22 @@ def tile_list_channel_shoal_outlook_kernel(
                 out=v_s[32 * q : 32 * q + 4, a, :].bitcast(I32),
                 in_=v_rows[64 * a + 16 * q : 64 * a + 16 * q + 16 : 4, :].bitcast(I32),
             )
-        swell_raw = sb("swell_raw", [P, PACK, PAIRS], F32, "pick0")
-        nc.sync.dma_start(out=swell_raw[:], in_=swell.rearrange("(p j) c -> p j c", j=PACK))
-        load_bias(1)
         raw01 = load_w1(0, 1, 0, PASS)
+        load_bias(1)
+        raw11 = load_w1(1, 1, 0, PASS)
+        swell_raw = sb("swell_raw", [P, PACK, PAIRS], F32)
+        nc.sync.dma_start(out=swell_raw[:], in_=swell.rearrange("(p j) c -> p j c", j=PACK))
         load_bias(2)
         load_bias(3)
+        load_per_row(gain_t, gain)
         for q in range(4):
             nc.sync.dma_start(
                 out=w_s[32 * q : 32 * q + 4, 2, :].bitcast(I32),
                 in_=w3_scales[0, 4 * q : 4 * q + 4, :].bitcast(I32),
             )
-        raw11 = load_w1(1, 1, 0, PASS)
         nc.sync.dma_start(
             out=w3_w[:].bitcast(I32), in_=w3_words[0].rearrange("p n t -> p (n t)").bitcast(I32)
         )
-        load_per_row(gain_t, gain)
         nc.sync.dma_start(
             out=w2_w[:].bitcast(I32), in_=w2_words.rearrange("a p c -> p a c").bitcast(I32)
         )
@@ -220,13 +219,23 @@ def tile_list_channel_shoal_outlook_kernel(
                 )
                 sums.setdefault((2 * k + u, lo), total[:, u, :])
 
-        def apply_gain(s, lo, hi):
+        def apply_gain(s, lo, hi, on_gpsimd=False):
             b, t = divmod(s, PACK)
             base = lo if (s, lo) in sums else 0
             if (b, lo) not in x_planes:
                 name = "x_planes%d_%d" % (b, lo)
                 tile = sb(name, [P, PACK, hi - lo], BF16, "w1_g11" if b == 0 else None)
                 x_planes.setdefault((b, lo), tile)
+            if on_gpsimd:
+                nc.gpsimd.tensor_scalar(
+                    out=x_planes[b, lo][:, t, :],
+                    in0=sums[s, base][:, lo - base : hi - base],
+                    scalar1=gain_t[:, s : s + 1],
+                    scalar2=0.0,
+                    op0=ALU.mult,
+                    op1=ALU.add,
+                )
+                return
             nc.scalar.activation(
                 out=x_planes[b, lo][:, t, :],
                 in_=sums[s, base][:, lo - base : hi - base],
@@ -303,19 +312,19 @@ def tile_list_channel_shoal_outlook_kernel(
         quantize_w1(1, 0, P, PASS)
 
         first_stage(0)
-        interleave(nc.vector.tensor_copy, swell_g[:], swell_raw[:])
+        group_w1(nc.vector.tensor_copy, 0, 1, raw01, 0, 0, PASS)
         first_stage(1)
-        picked = pick_first(0, 0, PAIRS, "pick0")
-        quantize(swell_c, swell_s, swell_g, 0, PAIRS)
+        picked = pick_first(0, 0, PAIRS, "w1_raw01_0")
+        quantize_w1(0, 1, 0, PASS)
         pick_second(0, 0, PAIRS, picked, None)
         first_stage(2)
         first_stage(3)
-        picked = pick_first(1, 0, PAIRS, None)
-        group_w1(scalar_round, 0, 1, raw01, 0, 0, PASS)
-        quantize_w1(0, 1, 0, PASS)
         group_w1(scalar_round, 1, 1, raw11, 0, 0, PASS)
         quantize_w1(1, 1, 0, PASS)
-        pick_second(1, 0, PAIRS, picked, "w1_raw11_0")
+        picked = pick_first(1, 0, PAIRS, "w1_raw11_0")
+        interleave(nc.scalar.copy, swell_g[:], swell_raw[:])
+        quantize(swell_c, swell_s, swell_g, 0, PAIRS)
+        pick_second(1, 0, PAIRS, picked, "swell_raw")
         first_stage(4)
         first_stage(5)
         pick_second(2, 0, PAIRS, pick_first(2, 0, PAIRS, None), "b1_2")
@@ -324,18 +333,20 @@ def tile_list_channel_shoal_outlook_kernel(
         first_stage(6)
         first_stage(7)
         for s in range(PACK):
-            apply_gain(s, 0, PAIRS)
+            apply_gain(s, 0, PAIRS, True)
+        for s in (4, 5):
+            apply_gain(s, *PIECES[0], True)
         pick_second(3, *PIECES[0], pick_first(3, *PIECES[0], None), "b1_3")
-        x_g.setdefault((0, 0), sb("x_g0_0", [P, PACK * PAIRS], BF16))
-        cut = X_SPLIT
-        interleave(nc.scalar.copy, x_g[0, 0][:, : PACK * cut], x_planes[0, 0][:, :, :cut])
-        interleave(nc.vector.tensor_copy, x_g[0, 0][:, PACK * cut :], x_planes[0, 0][:, :, cut:])
+        group_x(nc.scalar.copy, 0, 0, PAIRS)
+        for piece in PIECES[1:]:
+            for s in (4, 5):
+                apply_gain(s, *piece)
         quantize_x(0, 0, PAIRS)
         for h in range(2):
             second_stage(0, h * HALF, (h + 1) * HALF)
 
         def close_piece(copy, lo, hi):
-            for s in range(PACK, 2 * PACK):
+            for s in (6, 7):
                 apply_gain(s, lo, hi)
             group_x(copy, 1, lo, hi)
             quantize_x(1, lo, hi)

from contextlib import ExitStack

import concourse.mybir as mybir

K, T, S, PAIRS, H, M, N = 1024, 4096, 1024, 512, 1024, 512, 768
FLOPS = 2 * (K * H * S + H * N * PAIRS + M * N * PAIRS)

F32 = mybir.dt.float32
BF16 = mybir.dt.bfloat16
I32 = mybir.dt.int32
U32 = mybir.dt.uint32
U16 = mybir.dt.uint16
U8 = mybir.dt.uint8
FP8X4 = mybir.dt.float8_e4m3fn_x4
FP4X4 = mybir.dt.float4_e2m1fn_x4
ACT = mybir.ActivationFunctionType
ALU = mybir.AluOpType

P = 128
PACK = 4
PASS = P * PACK
BANK = 512
HALF = PAIRS // 2
N_TILES = N // P
PIECES = ((0, 256), (256, 384), (384, 512))


def tile_list_channel_shoal_outlook_kernel(
    tc, tab_words, tab_scales, offs, pos1, pos2, w1, b1, gain,
    w2_words, w2_scales, swell, w3_words, w3_scales, b2, out,
):
    nc = tc.nc
    with ExitStack() as ctx:
        keep = ctx.enter_context(tc.tile_pool(name="keep", bufs=1))
        psum = ctx.enter_context(tc.psum_pool(name="psum", bufs=1))

        def sb(name, shape, dtype, tag=None):
            return keep.tile(shape, dtype, name=name, tag=tag or name, align_bytes=64)

        def bank(index, name, shape):
            return psum.tile(shape, F32, name=name, tag="bank%d" % index)

        offs_t = keep.tile([P, S // 16], U16, name="offs_t")
        pos1_t = keep.tile([P, PAIRS // 16], U16, name="pos1_t")
        pos2_t = keep.tile([P, PAIRS // 16], U16, name="pos2_t")
        tab_w = [sb("tab_w%d" % a, [P, T], U16) for a in range(2)]
        tab_s = sb("tab_s", [P, T], U8)
        v_rows = sb("v_rows", [P, S], U8)
        v_s = sb("v_s", [P, 2, S], U8)
        w_s = sb("w_s", [P, 3, N], U8)
        b1_t = [sb("b1_%d" % k, [P, 2], F32) for k in range(PACK)]
        gain_t = sb("gain_t", [P, 2 * PACK], F32)
        b2_t = sb("b2_t", [P, N_TILES], F32)
        w2_w = sb("w2_w", [P, 2, 2 * N], U8)
        w3_w = sb("w3_w", [P, N], U32)

        nc.vector.memset(tab_s[:].bitcast(I32), 0)
        nc.vector.memset(w_s[:].rearrange("p a n -> p (a n)").bitcast(I32), 0)
        nc.vector.memset(v_s[:].rearrange("p a n -> p (a n)").bitcast(I32), 0)

        def load_w1(a, b, c0, width, tag=None):
            raw = sb("w1_raw%d%d_%d" % (a, b, c0), [P, PACK, width], F32, tag)
            rows = w1[a * PASS : (a + 1) * PASS, b * PASS + c0 : b * PASS + c0 + width]
            nc.sync.dma_start(out=raw[:], in_=rows.rearrange("(p j) c -> p j c", j=PACK))
            return raw

        def load_per_row(tile, vec):
            nc.sync.dma_start(
                out=tile[:].rearrange("p (b t) -> p b t", t=PACK),
                in_=vec.rearrange("(b p t) -> p b t", p=P, t=PACK),
            )

        def load_bias(k):
            b, half = divmod(k, 2)
            by_row = b1.rearrange("(b p t) -> b p t", p=P, t=PACK)
            nc.sync.dma_start(out=b1_t[k][:], in_=by_row[b, :, 2 * half : 2 * half + 2])

        nc.sync.dma_start(offs_t[:], offs)
        nc.sync.dma_start(out=tab_w[0][:].bitcast(I32), in_=tab_words[0].bitcast(I32))
        nc.sync.dma_start(
            out=tab_s[0:P:4, :].bitcast(I32),
            in_=tab_scales.rearrange("a q t -> (a q) t").bitcast(I32),
        )
        nc.sync.dma_start(pos1_t[:], pos1)
        nc.sync.dma_start(pos2_t[:], pos2)
        load_bias(0)
        raw00 = load_w1(0, 0, 0, PASS)
        nc.sync.dma_start(out=tab_w[1][:].bitcast(I32), in_=tab_words[1].bitcast(I32))
        raw10 = [load_w1(1, 0, 0, PASS // 2)]
        raw10.append(load_w1(1, 0, PASS // 2, PASS // 2))

        def gather_table(dst, window):
            nc.vector.tensor_copy(dst[:], window[:].indirect(offs_t[:]))

        gather_table(v_rows, tab_s)
        v_w = [sb("v_w%d" % a, [P, S], U16, ("tab_s", None)[a]) for a in range(2)]
        gather_table(v_w[0], tab_w[0])
        gather_table(v_w[1], tab_w[1])
        for n in range(8):
            a, q = divmod(n, 4)
            queue = nc.sync if n < 6 else nc.gpsimd
            queue.dma_start(
                out=v_s[32 * q : 32 * q + 4, a, :].bitcast(I32),
                in_=v_rows[64 * a + 16 * q : 64 * a + 16 * q + 16 : 4, :].bitcast(I32),
            )
        raw01 = load_w1(0, 1, 0, PASS)
        load_bias(1)
        raw11 = load_w1(1, 1, 0, PASS)
        swell_raw = sb("swell_raw", [P, PACK, PAIRS], F32)
        nc.sync.dma_start(out=swell_raw[:], in_=swell.rearrange("(p j) c -> p j c", j=PACK))
        load_bias(2)
        load_bias(3)
        load_per_row(gain_t, gain)
        for q in range(4):
            nc.sync.dma_start(
                out=w_s[32 * q : 32 * q + 4, 2, :].bitcast(I32),
                in_=w3_scales[0, 4 * q : 4 * q + 4, :].bitcast(I32),
            )
        nc.sync.dma_start(
            out=w3_w[:].bitcast(I32), in_=w3_words[0].rearrange("p n t -> p (n t)").bitcast(I32)
        )
        nc.sync.dma_start(
            out=w2_w[:].bitcast(I32), in_=w2_words.rearrange("a p c -> p a c").bitcast(I32)
        )
        for q in range(4):
            nc.sync.dma_start(
                out=w_s[32 * q : 32 * q + 4, 0:2, :].bitcast(I32),
                in_=w2_scales[:, 4 * q : 4 * q + 4, :].rearrange("a r n -> r a n").bitcast(I32),
            )
        with nc.allow_non_contiguous_dma(reason="one bias value for each output row"):
            nc.sync.dma_start(out=b2_t[:], in_=b2.rearrange("(i p) -> p i", p=P))

        w1_g = {}
        w1_c = {}
        w1_s = {}
        for a in range(2):
            for b in range(2):
                w1_g.setdefault((a, b), sb("w1_g%d%d" % (a, b), [P, PACK * PASS], BF16))
                w1_c.setdefault((a, b), sb("w1_c%d%d" % (a, b), [P, PASS], U32))
                w1_s.setdefault((a, b), sb("w1_s%d%d" % (a, b), [P, PASS], U8))

        def scalar_round(out, in_):
            nc.scalar.activation(out=out, in_=in_, func=ACT.Copy)

        def group_w1(copy, a, b, raw, c0, lo, hi):
            dst = w1_g[a, b][:].rearrange("p (t m j) -> p m t j", t=PACK, j=PACK)
            copy(
                out=dst[:, (c0 + lo) // PACK : (c0 + hi) // PACK],
                in_=raw[:, :, lo:hi].rearrange("p j (m t) -> p m t j", t=PACK),
            )

        def quantize(codes, scales, grouped, lo, hi):
            nc.vector.quantize_mx(
                out=codes[:, lo:hi].bitcast(FP8X4),
                scales=scales[:, lo:hi],
                in_=grouped[:, PACK * lo : PACK * hi],
            )

        def quantize_w1(a, b, lo, hi):
            quantize(w1_c[a, b], w1_s[a, b], w1_g[a, b], lo, hi)

        def interleave(copy, grouped, planes):
            copy(
                out=grouped.rearrange("p (c i t) -> p c t i", i=4, t=PACK),
                in_=planes.rearrange("p t (c i) -> p c t i", i=4),
            )

        gelu_t = [sb("gelu%d" % s, [P, S], F32) for s in range(2 * PACK)]

        def first_stage(s):
            b, t = divmod(s, PACK)
            cols = slice(t * P, (t + 1) * P)
            accs = [bank(2 * (s % 2) + u, "e%d_%d" % (s, u), [P, BANK]) for u in range(2)]
            if s == 0:
                order = [(a, u) for a in (0, 1) for u in range(2)]
            else:
                order = [(a, u) for u in range(2) for a in (1, 0)]
            for a, u in order:
                if True:
                    nc.tensor.matmul_mx(
                        out=accs[u][:],
                        lhsT=w1_c[a, b][:, cols].bitcast(FP8X4),
                        lhsT_scale=w1_s[a, b][:, cols],
                        rhs=v_w[a][:, u * BANK : (u + 1) * BANK].bitcast(FP4X4),
                        rhs_scale=v_s[:, a, u * BANK : (u + 1) * BANK],
                        start=(a == order[0][0]),
                        stop=(a != order[0][0]),
                    )
            for u in range(2):
                nc.scalar.activation(
                    out=gelu_t[s][:, u * BANK : (u + 1) * BANK],
                    in_=accs[u][:],
                    func=ACT.Gelu_apprx_tanh,
                    bias=b1_t[s // 2][:, s % 2 : s % 2 + 1],
                )

        sums = {}
        x_planes = {}
        x_g = {}
        x_c = [sb("x_c%d" % b, [P, PAIRS], U32) for b in range(2)]
        x_s = [sb("x_s%d" % b, [P, PAIRS], U8) for b in range(2)]

        def pick_first(k, lo, hi, tag):
            picked = sb("picked%d_%d" % (k, lo), [P, 2, hi - lo], F32, tag)
            for u in range(2):
                window = gelu_t[2 * k + u][:]
                nc.vector.tensor_copy(picked[:, u, :], window.indirect(pos1_t[:, lo // 16 : hi // 16]))
            return picked

        def pick_second(k, lo, hi, picked, tag):
            total = sb("sums%d_%d" % (k, lo), [P, 2, hi - lo], F32, tag)
            for u in range(2):
                window = gelu_t[2 * k + u][:]
                nc.vector.tensor_tensor(
                    total[:, u, :],
                    window.indirect(pos2_t[:, lo // 16 : hi // 16]),
                    picked[:, u, :],
                    ALU.add,
                )
                sums.setdefault((2 * k + u, lo), total[:, u, :])

        def apply_gain(s, lo, hi, on_gpsimd=False):
            b, t = divmod(s, PACK)
            base = lo if (s, lo) in sums else 0
            if (b, lo) not in x_planes:
                name = "x_planes%d_%d" % (b, lo)
                tile = sb(name, [P, PACK, hi - lo], BF16, "w1_g11" if b == 0 else None)
                x_planes.setdefault((b, lo), tile)
            if on_gpsimd:
                nc.gpsimd.tensor_scalar(
                    out=x_planes[b, lo][:, t, :],
                    in0=sums[s, base][:, lo - base : hi - base],
                    scalar1=gain_t[:, s : s + 1],
                    scalar2=0.0,
                    op0=ALU.mult,
                    op1=ALU.add,
                )
                return
            nc.scalar.activation(
                out=x_planes[b, lo][:, t, :],
                in_=sums[s, base][:, lo - base : hi - base],
                func=ACT.Copy,
                scale=gain_t[:, s : s + 1],
            )

        def group_x(copy, b, lo, hi):
            x_g.setdefault((b, lo), sb("x_g%d_%d" % (b, lo), [P, PACK * (hi - lo)], BF16))
            interleave(copy, x_g[b, lo][:], x_planes[b, lo][:])

        def quantize_x(b, lo, hi):
            quantize(x_c[b][:, lo:hi], x_s[b][:, lo:hi], x_g[b, lo], 0, hi - lo)

        swell_g = sb("swell_g", [P, PACK * PAIRS], BF16)
        swell_c = sb("swell_c", [P, PAIRS], U32)
        swell_s = sb("swell_s", [P, PAIRS], U8)
        f_t = [sb("f%d" % i, [P, PAIRS], F32) for i in range(N_TILES)]

        def swell_features(i):
            acc = bank(4 + i % 4, "f_acc%d" % i, [P, PAIRS])
            nc.tensor.matmul_mx(
                out=acc[:],
                lhsT=w3_w[:, i * P : (i + 1) * P].bitcast(FP8X4),
                lhsT_scale=w_s[:, 2, i * P : (i + 1) * P],
                rhs=swell_c[:].bitcast(FP8X4),
                rhs_scale=swell_s[:],
                start=True,
                stop=True,
            )
            nc.scalar.copy(out=f_t[i][:], in_=acc[:])

        y_acc = {}
        y_banks = (4, 5, 6, 7, 0, 2)

        def second_stage(b, lo, hi):
            h = lo // HALF
            for g in range(N_TILES // 2):
                if b == 0:
                    acc = bank(y_banks[3 * h + g], "y%d_%d" % (h, g), [P, 2, HALF])
                    y_acc.setdefault((h, g), acc)
                for u in range(2):
                    i = 2 * g + u
                    nc.tensor.matmul_mx(
                        out=y_acc[h, g][:, u, lo - h * HALF : hi - h * HALF],
                        lhsT=w2_w[:, b, 2 * i * P : 2 * (i + 1) * P].bitcast(FP4X4),
                        lhsT_scale=w_s[:, b, i * P : (i + 1) * P],
                        rhs=x_c[b][:, lo:hi].bitcast(FP8X4),
                        rhs_scale=x_s[b][:, lo:hi],
                        start=(b == 0 and u == 0),
                        stop=(b == 1 and u == 1 and hi % HALF == 0),
                    )

        def finish(h):
            cols = slice(h * HALF, (h + 1) * HALF)
            for i in range(N_TILES):
                res = sb("res%d_%d" % (h, i), [P, HALF], F32)
                nc.vector.scalar_tensor_tensor(
                    out=res[:],
                    in0=y_acc[h, i // 2][:, i % 2, :],
                    scalar=b2_t[:, i : i + 1],
                    in1=f_t[i][:, cols],
                    op0=ALU.add,
                    op1=ALU.max,
                )
                nc.sync.dma_start(out=out[i * P : (i + 1) * P, cols], in_=res[:])

        group_w1(scalar_round, 0, 0, raw00, 0, 0, PASS)
        group_w1(scalar_round, 1, 0, raw10[0], 0, 0, PASS // 2)
        quantize_w1(0, 0, 0, P)
        group_w1(nc.vector.tensor_copy, 1, 0, raw10[1], PASS // 2, 0, PASS // 2)
        quantize_w1(1, 0, 0, P)
        quantize_w1(0, 0, P, PASS)
        quantize_w1(1, 0, P, PASS)

        first_stage(0)
        group_w1(nc.vector.tensor_copy, 0, 1, raw01, 0, 0, PASS)
        first_stage(1)
        picked = pick_first(0, 0, PAIRS, "w1_raw01_0")
        quantize_w1(0, 1, 0, PASS)
        pick_second(0, 0, PAIRS, picked, None)
        first_stage(2)
        first_stage(3)
        group_w1(scalar_round, 1, 1, raw11, 0, 0, PASS)
        quantize_w1(1, 1, 0, PASS)
        picked = pick_first(1, 0, PAIRS, "w1_raw11_0")
        interleave(nc.scalar.copy, swell_g[:], swell_raw[:])
        quantize(swell_c, swell_s, swell_g, 0, PAIRS)
        pick_second(1, 0, PAIRS, picked, "swell_raw")
        first_stage(4)
        first_stage(5)
        pick_second(2, 0, PAIRS, pick_first(2, 0, PAIRS, None), "b1_2")
        for i in range(N_TILES):
            swell_features(i)
        first_stage(6)
        first_stage(7)
        for s in range(PACK):
            apply_gain(s, 0, PAIRS, True)
        for s in (4, 5):
            apply_gain(s, *PIECES[0], True)
        pick_second(3, *PIECES[0], pick_first(3, *PIECES[0], None), "b1_3")
        group_x(nc.scalar.copy, 0, 0, PAIRS)
        for piece in PIECES[1:]:
            for s in (4, 5):
                apply_gain(s, *piece)
        quantize_x(0, 0, PAIRS)
        for h in range(2):
            second_stage(0, h * HALF, (h + 1) * HALF)

        def close_piece(copy, lo, hi):
            for s in (6, 7):
                apply_gain(s, lo, hi)
            group_x(copy, 1, lo, hi)
            quantize_x(1, lo, hi)
            second_stage(1, lo, hi)

        pick_second(3, *PIECES[1], pick_first(3, *PIECES[1], "w1_g11"), None)
        close_piece(nc.scalar.copy, *PIECES[0])
        pick_second(3, *PIECES[2], pick_first(3, *PIECES[2], "x_planes1_0"), None)
        close_piece(nc.scalar.copy, *PIECES[1])
        close_piece(nc.scalar.copy, *PIECES[2])
        for h in range(2):
            finish(h)
